import numpy as np
import ml_dtypes


def mxq(x, axis, fmt="e4m3"):
    dtype, down = {"e4m3": (ml_dtypes.float8_e4m3fn, 7), "e5m2": (ml_dtypes.float8_e5m2, 14)}[fmt]
    v = np.moveaxis(np.asarray(x, np.float32).astype(ml_dtypes.bfloat16).astype(np.float64), axis, -1)
    blocks = v.reshape(v.shape[:-1] + (-1, 32))
    amax = np.abs(blocks).max(-1, keepdims=True)
    byte = np.maximum(np.where(amax > 0, np.frexp(amax)[1] - 1 + 127, 0) - down, 1)
    scale = np.exp2(byte - 127.0)
    codes = (blocks / scale).astype(np.float32).astype(dtype).astype(np.float64)
    return np.moveaxis((codes * scale).reshape(v.shape), -1, axis)


WIDE = False


def mx_kscale(k):
    if not WIDE:
        return np.ones(k)
    levels = np.array([10, -10, 5, -5, 0])
    if k % 512:
        return np.exp2(np.random.permutation(np.resize(levels, k // 32))).repeat(32)
    a = np.empty((k // 512, 16))
    for p in range(k // 512):
        a[p, :8] = np.random.permutation(np.resize(levels, 8))
        for g in range(8):
            far = levels[np.abs(levels - a[p, g]) >= 10]
            a[p, g + 8] = far[np.random.randint(len(far))]
    return np.exp2(a.ravel()).repeat(32)


def f64(x):
    return np.asarray(x).astype(np.float64)


def striped(idx):
    return np.tile(idx.reshape(-1, 16).T, (8, 1)).astype(np.uint16)


def unstriped(offs):
    return offs[:16].T.reshape(-1).astype(np.int64)


def pack_weight(w):
    k, n = w.shape
    w = f64(np.asarray(w, np.float32).astype(ml_dtypes.bfloat16)).reshape(k // 32, 32, n)
    amax = np.abs(w).max(1)
    byte = np.clip(np.where(amax > 0, np.frexp(amax)[1] - 1 + 127 - 7, 1), 1, 254)
    scaled = (w * np.exp2(127.0 - byte)[:, None, :]).reshape(k, n).astype(np.float32)
    words = np.ascontiguousarray(scaled.reshape(k // 512, 128, 4, n).transpose(0, 1, 3, 2)).astype(ml_dtypes.float8_e4m3fn).view(np.uint8)
    return words, np.ascontiguousarray(byte.astype(np.uint8).reshape(k // 512, 16, n))


def unpack_weight(words, scales):
    g, p, n, _ = words.shape
    vals = np.ascontiguousarray(words).view(ml_dtypes.float8_e4m3fn).astype(np.float64) * np.repeat(np.exp2(scales.astype(np.float64) - 127.0), 8, axis=1)[..., None]
    return vals.transpose(0, 1, 3, 2).reshape(g * 512, n)


K, T, S, N, H, W, C = 512, 2048, 512, 512, 512, 2048, 512


def setup_inputs():
    n = np.random.standard_normal
    s = mx_kscale(K)[:, None]
    u = mx_kscale(S)
    packed_xT = pack_weight(n((K, T)) * s)
    return {
        "x_words": packed_xT[0],
        "x_scales": packed_xT[1],
        "w1": (n((K, H)) / np.sqrt(K) / s).astype(np.float32),
        "gn": (np.random.uniform(0.5, 1.5, (H, 1)) * u[:, None]).astype(np.float32),
        "w2": (n((H, N)) / np.sqrt(H) / u[:, None]).astype(np.float32),
        "gs": (np.random.uniform(0.5, 1.5, (K, 1)) / s).astype(np.float32),
        "offs": striped(np.random.permutation(T)[:S]),
        "n1": striped(np.random.permutation(S)),
        "n2": striped(np.random.permutation(S)),
        "n3": striped(np.random.randint(0, S, W)),
        "cand": striped(np.random.permutation(T)[:C]),
        "n4": striped(np.random.permutation(S)),
        "n5": striped(np.random.permutation(S)),
    }


def reference(x_words, x_scales, w1, gn, w2, gs, offs, n1, n2, n3, cand, n4, n5):
    xq = unpack_weight(x_words, x_scales)[:, unstriped(offs)]
    y = mxq(f64(w1), 0, "e4m3").T @ xq
    z = f64(gn) * (y[:, unstriped(n1)] - y[:, unstriped(n2)])
    a = mxq(f64(w2), 0, "e4m3").T @ mxq(z, 0, "e4m3")
    x_cand = unpack_weight(x_words, x_scales)[:, unstriped(cand)]
    mb = y[:, unstriped(n3)]
    mn = mb.reshape(H, S, 4).min(axis=2)
    mx = mb.reshape(H, S, 4).max(axis=2)
    z2 = f64(gs) * (np.maximum(y, mn) - (0.5 * mx))
    b = 0.0625 * ((x_cand.T @ mxq(z2, 0, "e4m3")))
    return (a - a[:, unstriped(n4)]) / (np.abs(b) + np.abs(b[:, unstriped(n5)]) + 0.5)

@@ -1,0 +1,211 @@
+from contextlib import ExitStack
+
+import concourse.mybir as mybir
+
+K, T, S, N, H, W, C = 512, 2048, 512, 512, 512, 2048, 512
+FLOPS = 2 * K * H * S + 2 * H * N * S + 2 * K * C * S
+
+F32 = mybir.dt.float32
+BF16 = mybir.dt.bfloat16
+I32 = mybir.dt.int32
+U32 = mybir.dt.uint32
+U16 = mybir.dt.uint16
+U8 = mybir.dt.uint8
+FP8X4 = mybir.dt.float8_e4m3fn_x4
+ALU = mybir.AluOpType
+ACT = mybir.ActivationFunctionType
+
+P = 128
+PACK = 4
+TILES = 4
+HALF = S // 2
+WIN = 528
+
+
+def tile_picked_fkcdnormbgapgmid_none_p_kernel(
+    tc, x_words, x_scales, w1, gn, w2, gs, offs, n1, n2, n3, cand, n4, n5, out
+):
+    nc = tc.nc
+    with ExitStack() as ctx:
+        keep = ctx.enter_context(tc.tile_pool(name="keep", bufs=1))
+        ring = ctx.enter_context(tc.tile_pool(name="ring", bufs=2))
+        psum = ctx.enter_context(tc.psum_pool(name="psum", bufs=1))
+
+        def load_list(name, src):
+            lst = keep.tile(list(src.shape), U16, name=name)
+            nc.sync.dma_start(lst[:], src)
+            return lst
+
+        def mx_tiles(name):
+            words = keep.tile([P, 512], U32, name=name + "_words", align_bytes=64)
+            scales = keep.tile([P, 512], U8, name=name + "_scales", align_bytes=64)
+            return words, scales
+
+        xs = keep.tile([P, T], U8, name="xs", align_bytes=64)
+        nc.vector.memset(xs[:].bitcast(I32), 0)
+        w1_rows = w1.rearrange("(p j) c -> p j c", j=PACK)
+        w1_raw = [keep.tile([P, PACK, H // 2], F32, name="w1_raw%d" % h) for h in range(2)]
+        nc.sync.dma_start(w1_raw[0][:], w1_rows[:, :, 0 : H // 2])
+        for q in range(4):
+            nc.sync.dma_start(
+                xs[32 * q : 32 * q + 4, :].bitcast(I32), x_scales[0, 4 * q : 4 * q + 4, :].bitcast(I32)
+            )
+        offs_t = load_list("offs_t", offs)
+        nc.sync.dma_start(w1_raw[1][:], w1_rows[:, :, H // 2 : H])
+        xw = keep.tile([P, T], I32, name="xw", align_bytes=64)
+        nc.sync.dma_start(xw[:], x_words[0].rearrange("p c r -> p (c r)").bitcast(I32))
+        cand_t = load_list("cand_t", cand)
+        n2_t = load_list("n2_t", n2)
+        n1_t = load_list("n1_t", n1)
+        w2_raw = keep.tile([P, PACK, N], F32, name="w2_raw")
+        nc.sync.dma_start(w2_raw[:], w2.rearrange("(p j) c -> p j c", j=PACK))
+        gn_t = keep.tile([P, PACK], F32, name="gn_t")
+        nc.sync.dma_start(gn_t[:], gn.rearrange("(p t) o -> p (t o)", t=PACK))
+        n3_t = load_list("n3_t", n3)
+        gs_t = keep.tile([P, PACK], F32, name="gs_t")
+        nc.sync.dma_start(gs_t[:], gs.rearrange("(p t) o -> p (t o)", t=PACK))
+        n4_t = load_list("n4_t", n4)
+        n5_t = load_list("n5_t", n5)
+
+        y_win = [keep.tile([P, WIN], F32, name="y_win%d" % t) for t in range(TILES)]
+        a_win = [keep.tile([P, WIN], F32, name="a_win%d" % i) for i in range(TILES)]
+        b_win = [keep.tile([P, WIN], F32, name="b_win%d" % i) for i in range(TILES)]
+        for win in y_win + a_win + b_win:
+            nc.gpsimd.memset(win[:, S:], 0.0)
+
+        w1_b = keep.tile([P, TILES, P, PACK], BF16, name="w1_b", align_bytes=64)
+        for h in range(2):
+            nc.scalar.copy(
+                w1_b[:, :, 64 * h : 64 * h + 64, :].rearrange("p t m j -> p m j t"),
+                w1_raw[h][:].rearrange("p j (m t) -> p m j t", t=TILES),
+            )
+        xo_w, xo_s = mx_tiles("xo")
+        xc_w, xc_s = mx_tiles("xc")
+        nc.vector.tensor_copy(xo_s[:], xs[:].indirect(offs_t[:]))
+        w1_w, w1_s = mx_tiles("w1")
+        nc.vector.quantize_mx(w1_w[:].bitcast(FP8X4), w1_s[:], w1_b[:].rearrange("p t m j -> p (t m j)"))
+        nc.vector.tensor_copy(xo_w[:], xw[:].bitcast(U32).indirect(offs_t[:]))
+        nc.vector.tensor_copy(xc_s[:], xs[:].indirect(cand_t[:]))
+
+        def product(bank, left, block, right):
+            cols = slice(P * block, P * (block + 1))
+            acc = psum.tile([P, S], F32, name=bank)
+            nc.tensor.matmul_mx(
+                acc[:],
+                lhsT=left[0][:, cols].bitcast(FP8X4),
+                lhsT_scale=left[1][:, cols],
+                rhs=right[0][:].bitcast(FP8X4),
+                rhs_scale=right[1][:],
+                start=True,
+                stop=True,
+            )
+            return acc
+
+        def weave(dst, src, gain):
+            nc.vector.tensor_tensor(
+                dst[:].rearrange("p (c i) t -> p c t i", i=2),
+                src[:].rearrange("p t (c i) -> p c t i", i=2),
+                gain[:].unsqueeze(1).unsqueeze(3).to_broadcast([P, S // 2, PACK, 2]),
+                ALU.mult,
+            )
+
+        def quantise(mx, src):
+            nc.vector.quantize_mx(mx[0][:].bitcast(FP8X4), mx[1][:], src[:].rearrange("p c t -> p (c t)"))
+
+        y_ps = [product("bank%d" % t, (w1_w, w1_s), t, (xo_w, xo_s)) for t in range(TILES)]
+        nc.vector.tensor_copy(xc_w[:], xw[:].bitcast(U32).indirect(cand_t[:]))
+        w2_b = keep.tile([P, N, PACK], BF16, name="w2_b", align_bytes=64)
+        nc.vector.tensor_copy(
+            w2_b[:].rearrange("p (c i) j -> p c j i", i=4), w2_raw[:].rearrange("p j (c i) -> p c j i", i=4)
+        )
+
+        z_f = keep.tile([P, TILES, S], F32, name="z_f")
+        for t in range(TILES):
+            nc.scalar.copy(y_win[t][:, 0:S], y_ps[t][:])
+            minus_y2 = ring.tile([P, S], F32, name="minus_y2", bufs=4)
+            nc.scalar.activation(minus_y2[:], y_win[t][:].indirect(n2_t[:]), ACT.Copy, scale=-1.0)
+            nc.vector.tensor_tensor(z_f[:, t, :], y_win[t][:].indirect(n1_t[:]), minus_y2[:], ALU.add)
+            if t == 0:
+                w2_mx = mx_tiles("w2")
+                quantise(w2_mx, w2_b)
+        z_b = keep.tile([P, S, PACK], BF16, name="z_b", align_bytes=64)
+        z_mx = mx_tiles("z")
+        weave(z_b, z_f, gn_t)
+
+        z2_f = keep.tile([P, TILES, S], F32, name="z2_f")
+        z2_b = keep.tile([P, S, PACK], BF16, name="z2_b", align_bytes=64)
+        z2_mx = mx_tiles("z2")
+
+        def combine(t, largest, raised):
+            nc.vector.scalar_tensor_tensor(z2_f[:, t, :], largest[:], -0.5, raised[:], ALU.mult, ALU.add)
+
+        pending = None
+        for t in range(TILES):
+            members = ring.tile([P, S, 2, 2], F32, name="members", bufs=4)
+            flat = members[:].rearrange("p c a b -> p (c a b)")
+            for u in range(W // S):
+                nc.scalar.activation(
+                    flat[:, S * u : S * (u + 1)], y_win[t][:].indirect(n3_t[:, 32 * u : 32 * u + 32]), ACT.Copy
+                )
+            lo = ring.tile([P, S, 2], F32, name="lo")
+            hi = ring.tile([P, S, 2], F32, name="hi")
+            nc.vector.tensor_tensor(lo[:], members[:, :, 0, :], members[:, :, 1, :], ALU.min)
+            if t == 0:
+                quantise(z_mx, z_b)
+            else:
+                combine(*pending)
+            nc.vector.tensor_tensor(hi[:], members[:, :, 0, :], members[:, :, 1, :], ALU.max)
+            mn = ring.tile([P, S], F32, name="mn")
+            mx = ring.tile([P, S], F32, name="mx")
+            nc.vector.tensor_tensor(mn[:], lo[:, :, 0], lo[:, :, 1], ALU.min)
+            nc.vector.tensor_tensor(mx[:], hi[:, :, 0], hi[:, :, 1], ALU.max)
+            up = ring.tile([P, S], F32, name="up")
+            nc.vector.tensor_tensor(up[:], mn[:], y_win[t][:, 0:S], ALU.max)
+            pending = (t, mx, up)
+
+        a_ps = [product("bank%d" % (TILES + i), w2_mx, i, z_mx) for i in range(TILES)]
+        a4 = keep.tile([P, TILES, S], F32, name="a4")
+        for i in range(TILES):
+            nc.scalar.copy(a_win[i][:, 0:S], a_ps[i][:])
+            nc.scalar.activation(a4[:, i, :], a_win[i][:].indirect(n4_t[:]), ACT.Copy)
+        num = keep.tile([P, TILES, S], F32, name="num")
+
+        def numerator(i):
+            nc.vector.tensor_tensor(num[:, i, :], a_ps[i][:], a4[:, i, :], ALU.subtract)
+
+        numerator(0)
+        combine(*pending)
+        numerator(1)
+        weave(z2_b, z2_f, gs_t)
+        numerator(2)
+        quantise(z2_mx, z2_b)
+        numerator(3)
+
+        b_ps = [product("bank%d" % i, (xc_w, xc_s), i, z2_mx) for i in range(TILES)]
+        inv = keep.tile([P, TILES, S], F32, name="inv")
+
+        def finish(i):
+            res = ring.tile([P, S], F32, name="res", bufs=4)
+            nc.vector.tensor_tensor(res[:], num[:, i, :], inv[:, i, :], ALU.mult)
+            nc.sync.dma_start(out[P * i : P * (i + 1), :], res[:])
+
+        def invert(i, den):
+            root = ring.tile([P, S], F32, name="root")
+            nc.scalar.activation(root[:], den[:], ACT.Abs_reciprocal_sqrt, bias=0.5, scale=0.0625)
+            nc.scalar.activation(inv[:, i, :], root[:], ACT.Square)
+
+        dens = []
+        for i in range(TILES):
+            nc.scalar.activation(b_win[i][:, 0:S], b_ps[i][:], ACT.Abs)
+            size = ring.tile([P, S], F32, name="size", bufs=4)
+            nc.scalar.activation(size[:], b_ps[i][:], ACT.Abs)
+            den = ring.tile([P, S], F32, name="den", bufs=4)
+            nc.vector.tensor_tensor(den[:], b_win[i][:].indirect(n5_t[:]), size[:], ALU.add)
+            dens.append(den)
+            if i >= 1:
+                invert(i - 1, dens[i - 1])
+            if i >= 2:
+                finish(i - 2)
+        invert(TILES - 1, dens[TILES - 1])
+        finish(TILES - 2)
+        finish(TILES - 1)

@@ -1,6 +1,7 @@
 from contextlib import ExitStack
 
 import concourse.mybir as mybir
+from concourse.masks import make_identity
 
 K, T, S, N, H, W, C = 512, 2048, 512, 512, 512, 2048, 512
 FLOPS = 2 * K * H * S + 2 * H * N * S + 2 * K * C * S
@@ -42,28 +43,26 @@ def tile_picked_fkcdnormbgapgmid_none_p_kernel(
             return words, scales
 
         xs = keep.tile([P, T], U8, name="xs", align_bytes=64)
-        nc.vector.memset(xs[:].bitcast(I32), 0)
-        w1_rows = w1.rearrange("(p j) c -> p j c", j=PACK)
-        w1_raw = [keep.tile([P, PACK, H // 2], F32, name="w1_raw%d" % h) for h in range(2)]
-        nc.sync.dma_start(w1_raw[0][:], w1_rows[:, :, 0 : H // 2])
+        nc.gpsimd.memset(xs[:].bitcast(I32), 0)
+        offs_t = load_list("offs_t", offs)
+        w1_raw = keep.tile([P, PACK, H], F32, name="w1_raw")
+        nc.sync.dma_start(w1_raw[:], w1.rearrange("(p j) c -> p j c", j=PACK))
+        n3_t = load_list("n3_t", n3)
         for q in range(4):
             nc.sync.dma_start(
                 xs[32 * q : 32 * q + 4, :].bitcast(I32), x_scales[0, 4 * q : 4 * q + 4, :].bitcast(I32)
             )
-        offs_t = load_list("offs_t", offs)
-        nc.sync.dma_start(w1_raw[1][:], w1_rows[:, :, H // 2 : H])
         xw = keep.tile([P, T], I32, name="xw", align_bytes=64)
         nc.sync.dma_start(xw[:], x_words[0].rearrange("p c r -> p (c r)").bitcast(I32))
+        gs_t = keep.tile([P, PACK], F32, name="gs_t")
+        nc.sync.dma_start(gs_t[:], gs.rearrange("(p t) o -> p (t o)", t=PACK))
         cand_t = load_list("cand_t", cand)
-        n2_t = load_list("n2_t", n2)
-        n1_t = load_list("n1_t", n1)
         w2_raw = keep.tile([P, PACK, N], F32, name="w2_raw")
         nc.sync.dma_start(w2_raw[:], w2.rearrange("(p j) c -> p j c", j=PACK))
         gn_t = keep.tile([P, PACK], F32, name="gn_t")
         nc.sync.dma_start(gn_t[:], gn.rearrange("(p t) o -> p (t o)", t=PACK))
-        n3_t = load_list("n3_t", n3)
-        gs_t = keep.tile([P, PACK], F32, name="gs_t")
-        nc.sync.dma_start(gs_t[:], gs.rearrange("(p t) o -> p (t o)", t=PACK))
+        n2_t = load_list("n2_t", n2)
+        n1_t = load_list("n1_t", n1)
         n4_t = load_list("n4_t", n4)
         n5_t = load_list("n5_t", n5)
 
@@ -72,20 +71,23 @@ def tile_picked_fkcdnormbgapgmid_none_p_kernel(
         b_win = [keep.tile([P, WIN], F32, name="b_win%d" % i) for i in range(TILES)]
         for win in y_win + a_win + b_win:
             nc.gpsimd.memset(win[:, S:], 0.0)
+        ident = keep.tile([P, P], F32, name="ident")
+        make_identity(nc, ident[:])
+        warm = keep.tile([P, 1], F32, name="warm")
+        nc.scalar.activation(warm[:], y_win[0][:, S : S + 1], ACT.Abs_reciprocal_sqrt, bias=0.5, scale=0.0625)
 
-        w1_b = keep.tile([P, TILES, P, PACK], BF16, name="w1_b", align_bytes=64)
-        for h in range(2):
-            nc.scalar.copy(
-                w1_b[:, :, 64 * h : 64 * h + 64, :].rearrange("p t m j -> p m j t"),
-                w1_raw[h][:].rearrange("p j (m t) -> p m j t", t=TILES),
-            )
         xo_w, xo_s = mx_tiles("xo")
         xc_w, xc_s = mx_tiles("xc")
+        w1_b = keep.tile([P, TILES, P, PACK], BF16, name="w1_b", align_bytes=64)
+        for h, copy in enumerate((nc.scalar.copy, nc.vector.tensor_copy)):
+            copy(
+                w1_b[:, :, 64 * h : 64 * h + 64, :].rearrange("p t m j -> p m j t"),
+                w1_raw[:, :, HALF * h : HALF * (h + 1)].rearrange("p j (m t) -> p m j t", t=TILES),
+            )
         nc.vector.tensor_copy(xo_s[:], xs[:].indirect(offs_t[:]))
-        w1_w, w1_s = mx_tiles("w1")
-        nc.vector.quantize_mx(w1_w[:].bitcast(FP8X4), w1_s[:], w1_b[:].rearrange("p t m j -> p (t m j)"))
+        w1_mx = mx_tiles("w1")
+        nc.vector.quantize_mx(w1_mx[0][:].bitcast(FP8X4), w1_mx[1][:], w1_b[:].rearrange("p t m j -> p (t m j)"))
         nc.vector.tensor_copy(xo_w[:], xw[:].bitcast(U32).indirect(offs_t[:]))
-        nc.vector.tensor_copy(xc_s[:], xs[:].indirect(cand_t[:]))
 
         def product(bank, left, block, right):
             cols = slice(P * block, P * (block + 1))
@@ -101,111 +103,163 @@ def tile_picked_fkcdnormbgapgmid_none_p_kernel(
             )
             return acc
 
-        def weave(dst, src, gain):
-            nc.vector.tensor_tensor(
-                dst[:].rearrange("p (c i) t -> p c t i", i=2),
-                src[:].rearrange("p t (c i) -> p c t i", i=2),
-                gain[:].unsqueeze(1).unsqueeze(3).to_broadcast([P, S // 2, PACK, 2]),
-                ALU.mult,
-            )
+        halves = [(slice(HALF * h, HALF * (h + 1)), slice(16 * h, 16 * h + 16)) for h in range(2)]
 
-        def quantise(mx, src):
-            nc.vector.quantize_mx(mx[0][:].bitcast(FP8X4), mx[1][:], src[:].rearrange("p c t -> p (c t)"))
+        def quantise_rows(mx, rows, gain, tag):
+            staged = [
+                keep.tile([P, HALF, PACK], BF16, name="%s%d" % (tag, h), tag="%s%d" % (tag, h), align_bytes=64)
+                for h in range(2)
+            ]
+            for h, (cols, part) in enumerate(halves):
+                nc.vector.tensor_tensor(
+                    staged[h][:].rearrange("p (c i) t -> p c t i", i=2),
+                    rows[:, :, cols].rearrange("p t (c i) -> p c t i", i=2),
+                    gain[:].unsqueeze(1).unsqueeze(3).to_broadcast([P, HALF // 2, PACK, 2]),
+                    ALU.mult,
+                )
+            for h, (cols, part) in enumerate(halves):
+                nc.vector.quantize_mx(
+                    mx[0][:, cols].bitcast(FP8X4), mx[1][:, cols], staged[h][:].rearrange("p c t -> p (c t)")
+                )
 
-        y_ps = [product("bank%d" % t, (w1_w, w1_s), t, (xo_w, xo_s)) for t in range(TILES)]
-        nc.vector.tensor_copy(xc_w[:], xw[:].bitcast(U32).indirect(cand_t[:]))
-        w2_b = keep.tile([P, N, PACK], BF16, name="w2_b", align_bytes=64)
-        nc.vector.tensor_copy(
-            w2_b[:].rearrange("p (c i) j -> p c j i", i=4), w2_raw[:].rearrange("p j (c i) -> p c j i", i=4)
-        )
+        def scalar_gather(dst, window, offsets):
+            nc.scalar.activation(dst, window[:].indirect(offsets), ACT.Copy)
 
-        z_f = keep.tile([P, TILES, S], F32, name="z_f")
-        for t in range(TILES):
-            nc.scalar.copy(y_win[t][:, 0:S], y_ps[t][:])
-            minus_y2 = ring.tile([P, S], F32, name="minus_y2", bufs=4)
-            nc.scalar.activation(minus_y2[:], y_win[t][:].indirect(n2_t[:]), ACT.Copy, scale=-1.0)
-            nc.vector.tensor_tensor(z_f[:, t, :], y_win[t][:].indirect(n1_t[:]), minus_y2[:], ALU.add)
-            if t == 0:
-                w2_mx = mx_tiles("w2")
-                quantise(w2_mx, w2_b)
-        z_b = keep.tile([P, S, PACK], BF16, name="z_b", align_bytes=64)
-        z_mx = mx_tiles("z")
-        weave(z_b, z_f, gn_t)
+        def vector_gather(dst, window, offsets):
+            nc.vector.tensor_copy(dst, window[:].indirect(offsets))
+
+        y_ps = [product("bank%d" % t, w1_mx, t, (xo_w, xo_s)) for t in range(TILES)]
+        members = [
+            keep.tile([P, HALF, 2, 2, 2], F32, name="members%d" % t, tag="members%d" % t, align_bytes=64)
+            for t in range(TILES)
+        ]
+
+        def fetch_members(t):
+            flat = members[t][:].rearrange("p c g a b -> p (c g a b)")
+            for u in range(W // S):
+                gather = vector_gather if t == 0 and u >= 2 else scalar_gather
+                gather(flat[:, S * u : S * (u + 1)], y_win[t], n3_t[:, 32 * u : 32 * u + 32])
 
         z2_f = keep.tile([P, TILES, S], F32, name="z2_f")
-        z2_b = keep.tile([P, S, PACK], BF16, name="z2_b", align_bytes=64)
-        z2_mx = mx_tiles("z2")
+        nc.scalar.copy(y_win[0][:, 0:S], y_ps[0][:])
+        nc.vector.tensor_copy(y_win[1][:, 0:S], y_ps[1][:])
 
         def combine(t, largest, raised):
             nc.vector.scalar_tensor_tensor(z2_f[:, t, :], largest[:], -0.5, raised[:], ALU.mult, ALU.add)
 
+        def fold_members(t, op, name):
+            folded = ring.tile([P, HALF, 2, 2], F32, name=name)
+            nc.vector.tensor_tensor(
+                folded[:].rearrange("p c b g -> p c g b"), members[t][:, :, :, 0, :], members[t][:, :, :, 1, :], op
+            )
+            return folded
+
+        def fold_pairs(folded, op, name):
+            single = ring.tile([P, HALF, 2], F32, name=name)
+            nc.vector.tensor_tensor(single[:], folded[:, :, 0, :], folded[:, :, 1, :], op)
+            return single[:].rearrange("p c g -> p (c g)")
+
         pending = None
         for t in range(TILES):
-            members = ring.tile([P, S, 2, 2], F32, name="members", bufs=4)
-            flat = members[:].rearrange("p c a b -> p (c a b)")
-            for u in range(W // S):
-                nc.scalar.activation(
-                    flat[:, S * u : S * (u + 1)], y_win[t][:].indirect(n3_t[:, 32 * u : 32 * u + 32]), ACT.Copy
-                )
-            lo = ring.tile([P, S, 2], F32, name="lo")
-            hi = ring.tile([P, S, 2], F32, name="hi")
-            nc.vector.tensor_tensor(lo[:], members[:, :, 0, :], members[:, :, 1, :], ALU.min)
-            if t == 0:
-                quantise(z_mx, z_b)
-            else:
+            if t > 1:
+                nc.scalar.copy(y_win[t][:, 0:S], y_ps[t][:])
+            fetch_members(t)
+            lo = fold_members(t, ALU.min, "lo")
+            if t > 0:
                 combine(*pending)
-            nc.vector.tensor_tensor(hi[:], members[:, :, 0, :], members[:, :, 1, :], ALU.max)
-            mn = ring.tile([P, S], F32, name="mn")
-            mx = ring.tile([P, S], F32, name="mx")
-            nc.vector.tensor_tensor(mn[:], lo[:, :, 0], lo[:, :, 1], ALU.min)
-            nc.vector.tensor_tensor(mx[:], hi[:, :, 0], hi[:, :, 1], ALU.max)
+            hi = fold_members(t, ALU.max, "hi")
+            mn = fold_pairs(lo, ALU.min, "mn")
+            mx = fold_pairs(hi, ALU.max, "mx")
             up = ring.tile([P, S], F32, name="up")
-            nc.vector.tensor_tensor(up[:], mn[:], y_win[t][:, 0:S], ALU.max)
+            nc.vector.tensor_tensor(up[:], mn, y_win[t][:, 0:S], ALU.max)
             pending = (t, mx, up)
+            if t == 1:
+                nc.vector.tensor_copy(xc_s[:], xs[:].indirect(cand_t[:]))
+            if t == 2:
+                nc.vector.tensor_copy(xc_w[:], xw[:].bitcast(U32).indirect(cand_t[:]))
 
-        a_ps = [product("bank%d" % (TILES + i), w2_mx, i, z_mx) for i in range(TILES)]
-        a4 = keep.tile([P, TILES, S], F32, name="a4")
-        for i in range(TILES):
-            nc.scalar.copy(a_win[i][:, 0:S], a_ps[i][:])
-            nc.scalar.activation(a4[:, i, :], a_win[i][:].indirect(n4_t[:]), ACT.Copy)
-        num = keep.tile([P, TILES, S], F32, name="num")
+        minus_y2 = keep.tile([P, TILES, S], F32, name="minus_y2")
+        for t in range(TILES):
+            nc.scalar.activation(minus_y2[:, t, :], y_win[t][:].indirect(n2_t[:]), ACT.Copy, scale=-1.0)
+        y1 = keep.tile([P, 2, S], F32, name="y1")
+        for t in range(2):
+            scalar_gather(y1[:, t, :], y_win[t], n1_t[:])
+        w2_b = keep.tile([P, N, PACK], BF16, name="w2_b", tag="members1", align_bytes=64)
+        nc.scalar.copy(
+            w2_b[:].rearrange("p (c i) j -> p c j i", i=4), w2_raw[:].rearrange("p j (c i) -> p c j i", i=4)
+        )
 
-        def numerator(i):
-            nc.vector.tensor_tensor(num[:, i, :], a_ps[i][:], a4[:, i, :], ALU.subtract)
-
-        numerator(0)
         combine(*pending)
-        numerator(1)
-        weave(z2_b, z2_f, gs_t)
-        numerator(2)
-        quantise(z2_mx, z2_b)
-        numerator(3)
+        z2_mx = mx_tiles("z2")
+        quantise_rows(z2_mx, z2_f, gs_t, "z2_b")
+        w2_w = keep.tile([P, N], U32, name="w2_w", tag="z2_b0", align_bytes=64)
+        w2_s = keep.tile([P, N], U8, name="w2_s", align_bytes=64)
+        z_f = keep.tile([P, TILES, S], F32, name="z_f", tag="z2_b1", align_bytes=64)
+        for t in range(TILES):
+            first = y1[:, t, :] if t < 2 else y_win[t][:].indirect(n1_t[:])
+            nc.vector.tensor_tensor(z_f[:, t, :], first, minus_y2[:, t, :], ALU.add)
+        nc.vector.quantize_mx(w2_w[:].bitcast(FP8X4), w2_s[:], w2_b[:].rearrange("p c t -> p (c t)"))
+        z_mx = mx_tiles("z")
+        quantise_rows(z_mx, z_f, gn_t, "z_b")
 
-        b_ps = [product("bank%d" % i, (xc_w, xc_s), i, z2_mx) for i in range(TILES)]
-        inv = keep.tile([P, TILES, S], F32, name="inv")
-
-        def finish(i):
-            res = ring.tile([P, S], F32, name="res", bufs=4)
-            nc.vector.tensor_tensor(res[:], num[:, i, :], inv[:, i, :], ALU.mult)
-            nc.sync.dma_start(out[P * i : P * (i + 1), :], res[:])
-
-        def invert(i, den):
-            root = ring.tile([P, S], F32, name="root")
-            nc.scalar.activation(root[:], den[:], ACT.Abs_reciprocal_sqrt, bias=0.5, scale=0.0625)
-            nc.scalar.activation(inv[:, i, :], root[:], ACT.Square)
-
-        dens = []
+        b_ps = [product("bank%d" % (TILES + i), (xc_w, xc_s), i, z2_mx) for i in range(TILES)]
         for i in range(TILES):
             nc.scalar.activation(b_win[i][:, 0:S], b_ps[i][:], ACT.Abs)
-            size = ring.tile([P, S], F32, name="size", bufs=4)
-            nc.scalar.activation(size[:], b_ps[i][:], ACT.Abs)
-            den = ring.tile([P, S], F32, name="den", bufs=4)
-            nc.vector.tensor_tensor(den[:], b_win[i][:].indirect(n5_t[:]), size[:], ALU.add)
-            dens.append(den)
-            if i >= 1:
-                invert(i - 1, dens[i - 1])
-            if i >= 2:
-                finish(i - 2)
-        invert(TILES - 1, dens[TILES - 1])
-        finish(TILES - 2)
-        finish(TILES - 1)
+
+        def denominator(i):
+            b5 = ring.tile([P, S], F32, name="b5", bufs=4)
+            scalar_gather(b5[:], b_win[i], n5_t[:])
+            den = psum.tile([P, S], F32, name="bank%d" % (TILES + i))
+            for j in range(TILES):
+                cols = slice(P * j, P * (j + 1))
+                nc.tensor.matmul(den[:, cols], b_win[i][:, cols], ident[:], start=True, stop=False, is_transpose=True)
+                nc.tensor.matmul(den[:, cols], b5[:, cols], ident[:], start=False, stop=True, is_transpose=True)
+            return den
+
+        def inverse_root(i):
+            root = ring.tile([P, S], F32, name="root", bufs=4)
+            nc.scalar.activation(root[:], den_ps[i][:], ACT.Abs_reciprocal_sqrt, bias=0.5, scale=0.0625)
+            return root
+
+        def inverse(i, root):
+            inv_t = ring.tile([P, S], F32, name="inv_t", bufs=4)
+            nc.scalar.activation(inv_t[:], root[:], ACT.Square)
+            return inv_t
+
+        def turn_back(i, inv_t):
+            inv = psum.tile([P, S], F32, name="bank%d" % i)
+            for j in range(TILES):
+                cols = slice(P * j, P * (j + 1))
+                nc.tensor.transpose(inv[:, cols], inv_t[:, cols], ident[:])
+            return inv
+
+        den_ps = [denominator(i) for i in range(TILES)]
+        roots = [inverse_root(i) for i in range(TILES)]
+        invs_t = [inverse(i, roots[i]) for i in range(TILES)]
+
+        a_ps = [product("bank%d" % i, (w2_w, w2_s), i, z_mx) for i in range(TILES)]
+        a4 = keep.tile([P, TILES, S], F32, name="a4")
+        for i in range(TILES):
+            if i < 2:
+                nc.vector.tensor_copy(a_win[i][:, 0:S], a_ps[i][:])
+            else:
+                nc.scalar.copy(a_win[i][:, 0:S], a_ps[i][:])
+        invs = [turn_back(i, invs_t[i]) for i in range(TILES)]
+        for i in range(TILES):
+            if i < 3:
+                for cols, part in halves:
+                    vector_gather(a4[:, i, cols], a_win[i], n4_t[:, part])
+            else:
+                scalar_gather(a4[:, i, :], a_win[i], n4_t[:])
+        nums = []
+        for i in range(TILES + 1):
+            if i < TILES:
+                num = ring.tile([P, S], F32, name="num", bufs=4)
+                nc.vector.tensor_tensor(num[:], a_win[i][:, 0:S], a4[:, i, :], ALU.subtract)
+                nums.append(num)
+            if i > 0:
+                res = ring.tile([P, S], F32, name="res", bufs=4)
+                pieces = [cols for cols, part in halves] if i == TILES else [slice(0, S)]
+                for cols in pieces:
+                    nc.vector.tensor_tensor(res[:, cols], nums[i - 1][:, cols], invs[i - 1][:, cols], ALU.mult)
+                    nc.sync.dma_start(out[P * (i - 1) : P * i, cols], res[:, cols])

@@ -21,6 +21,7 @@ PACK = 4
 TILES = 4
 HALF = S // 2
 WIN = 528
+Y_WIN = 1040
 
 
 def tile_picked_fkcdnormbgapgmid_none_p_kernel(
@@ -45,18 +46,18 @@ def tile_picked_fkcdnormbgapgmid_none_p_kernel(
         xs = keep.tile([P, T], U8, name="xs", align_bytes=64)
         nc.gpsimd.memset(xs[:].bitcast(I32), 0)
         offs_t = load_list("offs_t", offs)
-        w1_raw = keep.tile([P, PACK, H], F32, name="w1_raw")
-        nc.sync.dma_start(w1_raw[:], w1.rearrange("(p j) c -> p j c", j=PACK))
-        n3_t = load_list("n3_t", n3)
+        cand_t = load_list("cand_t", cand)
         for q in range(4):
             nc.sync.dma_start(
                 xs[32 * q : 32 * q + 4, :].bitcast(I32), x_scales[0, 4 * q : 4 * q + 4, :].bitcast(I32)
             )
+        w1_raw = keep.tile([P, PACK, H], F32, name="w1_raw")
+        nc.sync.dma_start(w1_raw[:], w1.rearrange("(p j) c -> p j c", j=PACK))
         xw = keep.tile([P, T], I32, name="xw", align_bytes=64)
         nc.sync.dma_start(xw[:], x_words[0].rearrange("p c r -> p (c r)").bitcast(I32))
+        n3_t = load_list("n3_t", n3)
         gs_t = keep.tile([P, PACK], F32, name="gs_t")
         nc.sync.dma_start(gs_t[:], gs.rearrange("(p t) o -> p (t o)", t=PACK))
-        cand_t = load_list("cand_t", cand)
         w2_raw = keep.tile([P, PACK, N], F32, name="w2_raw")
         nc.sync.dma_start(w2_raw[:], w2.rearrange("(p j) c -> p j c", j=PACK))
         gn_t = keep.tile([P, PACK], F32, name="gn_t")
@@ -66,7 +67,7 @@ def tile_picked_fkcdnormbgapgmid_none_p_kernel(
         n4_t = load_list("n4_t", n4)
         n5_t = load_list("n5_t", n5)
 
-        y_win = [keep.tile([P, WIN], F32, name="y_win%d" % t) for t in range(TILES)]
+        y_win = [keep.tile([P, Y_WIN], F32, name="y_win%d" % t) for t in range(TILES)]
         a_win = [keep.tile([P, WIN], F32, name="a_win%d" % i) for i in range(TILES)]
         b_win = [keep.tile([P, WIN], F32, name="b_win%d" % i) for i in range(TILES)]
         for win in y_win + a_win + b_win:
@@ -78,32 +79,33 @@ def tile_picked_fkcdnormbgapgmid_none_p_kernel(
 
         xo_w, xo_s = mx_tiles("xo")
         xc_w, xc_s = mx_tiles("xc")
+        nc.vector.tensor_copy(xo_s[:], xs[:].indirect(offs_t[:]))
+        nc.vector.tensor_copy(xc_s[:], xs[:].indirect(cand_t[:]))
         w1_b = keep.tile([P, TILES, P, PACK], BF16, name="w1_b", align_bytes=64)
         for h, copy in enumerate((nc.scalar.copy, nc.vector.tensor_copy)):
             copy(
                 w1_b[:, :, 64 * h : 64 * h + 64, :].rearrange("p t m j -> p m j t"),
                 w1_raw[:, :, HALF * h : HALF * (h + 1)].rearrange("p j (m t) -> p m j t", t=TILES),
             )
-        nc.vector.tensor_copy(xo_s[:], xs[:].indirect(offs_t[:]))
         w1_mx = mx_tiles("w1")
         nc.vector.quantize_mx(w1_mx[0][:].bitcast(FP8X4), w1_mx[1][:], w1_b[:].rearrange("p t m j -> p (t m j)"))
-        nc.vector.tensor_copy(xo_w[:], xw[:].bitcast(U32).indirect(offs_t[:]))
+        halves = [(slice(HALF * h, HALF * (h + 1)), slice(16 * h, 16 * h + 16)) for h in range(2)]
+        for cols, part in halves:
+            nc.vector.tensor_copy(xo_w[:, cols], xw[:].bitcast(U32).indirect(offs_t[:, part]))
 
-        def product(bank, left, block, right):
+        def product(bank, left, block, right, moving=slice(0, S)):
             cols = slice(P * block, P * (block + 1))
-            acc = psum.tile([P, S], F32, name=bank)
+            acc = psum.tile([P, moving.stop - moving.start], F32, name=bank)
             nc.tensor.matmul_mx(
                 acc[:],
                 lhsT=left[0][:, cols].bitcast(FP8X4),
                 lhsT_scale=left[1][:, cols],
-                rhs=right[0][:].bitcast(FP8X4),
-                rhs_scale=right[1][:],
+                rhs=right[0][:, moving].bitcast(FP8X4),
+                rhs_scale=right[1][:, moving],
                 start=True,
                 stop=True,
             )
             return acc
-
-        halves = [(slice(HALF * h, HALF * (h + 1)), slice(16 * h, 16 * h + 16)) for h in range(2)]
 
         def quantise_rows(mx, rows, gain, tag):
             staged = [
@@ -128,7 +130,8 @@ def tile_picked_fkcdnormbgapgmid_none_p_kernel(
         def vector_gather(dst, window, offsets):
             nc.vector.tensor_copy(dst, window[:].indirect(offsets))
 
-        y_ps = [product("bank%d" % t, w1_mx, t, (xo_w, xo_s)) for t in range(TILES)]
+        y0_ps = [product("bank%d" % (TILES * h), w1_mx, 0, (xo_w, xo_s), halves[h][0]) for h in range(2)]
+        y_ps = {t: product("bank%d" % t, w1_mx, t, (xo_w, xo_s)) for t in range(1, TILES)}
         members = [
             keep.tile([P, HALF, 2, 2, 2], F32, name="members%d" % t, tag="members%d" % t, align_bytes=64)
             for t in range(TILES)
@@ -136,13 +139,19 @@ def tile_picked_fkcdnormbgapgmid_none_p_kernel(
 
         def fetch_members(t):
             flat = members[t][:].rearrange("p c g a b -> p (c g a b)")
-            for u in range(W // S):
-                gather = vector_gather if t == 0 and u >= 2 else scalar_gather
-                gather(flat[:, S * u : S * (u + 1)], y_win[t], n3_t[:, 32 * u : 32 * u + 32])
+            split = W - S if t == 0 else W
+            for first in range(0, split, 2 * S):
+                last = min(first + 2 * S, split)
+                scalar_gather(flat[:, first:last], y_win[t], n3_t[:, first // 16 : last // 16])
+            if split < W:
+                vector_gather(flat[:, split:W], y_win[t], n3_t[:, split // 16 : W // 16])
+                nc.vector.tensor_copy(xc_w[:], xw[:].bitcast(U32).indirect(cand_t[:]))
 
         z2_f = keep.tile([P, TILES, S], F32, name="z2_f")
-        nc.scalar.copy(y_win[0][:, 0:S], y_ps[0][:])
-        nc.vector.tensor_copy(y_win[1][:, 0:S], y_ps[1][:])
+        for h, (cols, part) in enumerate(halves):
+            nc.scalar.copy(y_win[0][:, cols], y0_ps[h][:])
+        for t in range(1, TILES):
+            nc.vector.tensor_copy(y_win[t][:, 0:S], y_ps[t][:])
 
         def combine(t, largest, raised):
             nc.vector.scalar_tensor_tensor(z2_f[:, t, :], largest[:], -0.5, raised[:], ALU.mult, ALU.add)
@@ -161,8 +170,6 @@ def tile_picked_fkcdnormbgapgmid_none_p_kernel(
 
         pending = None
         for t in range(TILES):
-            if t > 1:
-                nc.scalar.copy(y_win[t][:, 0:S], y_ps[t][:])
             fetch_members(t)
             lo = fold_members(t, ALU.min, "lo")
             if t > 0:
@@ -173,10 +180,6 @@ def tile_picked_fkcdnormbgapgmid_none_p_kernel(
             up = ring.tile([P, S], F32, name="up")
             nc.vector.tensor_tensor(up[:], mn, y_win[t][:, 0:S], ALU.max)
             pending = (t, mx, up)
-            if t == 1:
-                nc.vector.tensor_copy(xc_s[:], xs[:].indirect(cand_t[:]))
-            if t == 2:
-                nc.vector.tensor_copy(xc_w[:], xw[:].bitcast(U32).indirect(cand_t[:]))
 
         minus_y2 = keep.tile([P, TILES, S], F32, name="minus_y2")
         for t in range(TILES):
@@ -234,8 +237,12 @@ def tile_picked_fkcdnormbgapgmid_none_p_kernel(
             return inv
 
         den_ps = [denominator(i) for i in range(TILES)]
-        roots = [inverse_root(i) for i in range(TILES)]
-        invs_t = [inverse(i, roots[i]) for i in range(TILES)]
+        roots = [inverse_root(0)]
+        invs_t = []
+        for i in range(TILES):
+            if i + 1 < TILES:
+                roots.append(inverse_root(i + 1))
+            invs_t.append(inverse(i, roots[i]))
 
         a_ps = [product("bank%d" % i, (w2_w, w2_s), i, z_mx) for i in range(TILES)]
         a4 = keep.tile([P, TILES, S], F32, name="a4")
@@ -246,20 +253,26 @@ def tile_picked_fkcdnormbgapgmid_none_p_kernel(
                 nc.scalar.copy(a_win[i][:, 0:S], a_ps[i][:])
         invs = [turn_back(i, invs_t[i]) for i in range(TILES)]
         for i in range(TILES):
-            if i < 3:
+            if i < 2:
                 for cols, part in halves:
                     vector_gather(a4[:, i, cols], a_win[i], n4_t[:, part])
             else:
                 scalar_gather(a4[:, i, :], a_win[i], n4_t[:])
-        nums = []
-        for i in range(TILES + 1):
-            if i < TILES:
-                num = ring.tile([P, S], F32, name="num", bufs=4)
-                nc.vector.tensor_tensor(num[:], a_win[i][:, 0:S], a4[:, i, :], ALU.subtract)
-                nums.append(num)
-            if i > 0:
-                res = ring.tile([P, S], F32, name="res", bufs=4)
-                pieces = [cols for cols, part in halves] if i == TILES else [slice(0, S)]
-                for cols in pieces:
-                    nc.vector.tensor_tensor(res[:, cols], nums[i - 1][:, cols], invs[i - 1][:, cols], ALU.mult)
-                    nc.sync.dma_start(out[P * (i - 1) : P * i, cols], res[:, cols])
+
+        def numerator(i):
+            num = ring.tile([P, S], F32, name="num", bufs=4)
+            nc.vector.tensor_tensor(num[:], a_win[i][:, 0:S], a4[:, i, :], ALU.subtract)
+            return num
+
+        def finish(i, num, pieces):
+            res = ring.tile([P, S], F32, name="res", bufs=4)
+            for cols in pieces:
+                nc.vector.tensor_tensor(res[:, cols], num[:, cols], invs[i][:, cols], ALU.mult)
+                nc.sync.dma_start(out[P * i : P * (i + 1), cols], res[:, cols])
+
+        whole = [slice(0, S)]
+        nums = [numerator(0), numerator(1)]
+        finish(0, nums[0], whole)
+        finish(1, nums[1], whole)
+        finish(2, numerator(2), whole)
+        finish(3, numerator(3), [cols for cols, part in halves])

@@ -56,10 +56,10 @@ def tile_picked_fkcdnormbgapgmid_none_p_kernel(
         xw = keep.tile([P, T], I32, name="xw", align_bytes=64)
         nc.sync.dma_start(xw[:], x_words[0].rearrange("p c r -> p (c r)").bitcast(I32))
         n3_t = load_list("n3_t", n3)
-        gs_t = keep.tile([P, PACK], F32, name="gs_t")
-        nc.sync.dma_start(gs_t[:], gs.rearrange("(p t) o -> p (t o)", t=PACK))
         w2_raw = keep.tile([P, PACK, N], F32, name="w2_raw")
         nc.sync.dma_start(w2_raw[:], w2.rearrange("(p j) c -> p j c", j=PACK))
+        gs_t = keep.tile([P, PACK], F32, name="gs_t")
+        nc.sync.dma_start(gs_t[:], gs.rearrange("(p t) o -> p (t o)", t=PACK))
         gn_t = keep.tile([P, PACK], F32, name="gn_t")
         nc.sync.dma_start(gn_t[:], gn.rearrange("(p t) o -> p (t o)", t=PACK))
         n2_t = load_list("n2_t", n2)
@@ -147,6 +147,11 @@ def tile_picked_fkcdnormbgapgmid_none_p_kernel(
                 vector_gather(flat[:, split:W], y_win[t], n3_t[:, split // 16 : W // 16])
                 nc.vector.tensor_copy(xc_w[:], xw[:].bitcast(U32).indirect(cand_t[:]))
 
+        w2_b = keep.tile([P, N, PACK], BF16, name="w2_b", align_bytes=64)
+        for cols, part in halves:
+            nc.gpsimd.tensor_scalar(
+                w2_b[:, cols, :], w2_raw[:, :, cols].rearrange("p j c -> p c j"), 1.0, 0.0, ALU.mult, ALU.add
+            )
         z2_f = keep.tile([P, TILES, S], F32, name="z2_f")
         for h, (cols, part) in enumerate(halves):
             nc.scalar.copy(y_win[0][:, cols], y0_ps[h][:])
@@ -181,16 +186,11 @@ def tile_picked_fkcdnormbgapgmid_none_p_kernel(
             nc.vector.tensor_tensor(up[:], mn, y_win[t][:, 0:S], ALU.max)
             pending = (t, mx, up)
 
-        minus_y2 = keep.tile([P, TILES, S], F32, name="minus_y2")
+        y1 = keep.tile([P, TILES, S], F32, name="y1")
+        y2 = keep.tile([P, TILES, S], F32, name="y2")
         for t in range(TILES):
-            nc.scalar.activation(minus_y2[:, t, :], y_win[t][:].indirect(n2_t[:]), ACT.Copy, scale=-1.0)
-        y1 = keep.tile([P, 2, S], F32, name="y1")
-        for t in range(2):
+            scalar_gather(y2[:, t, :], y_win[t], n2_t[:])
             scalar_gather(y1[:, t, :], y_win[t], n1_t[:])
-        w2_b = keep.tile([P, N, PACK], BF16, name="w2_b", tag="members1", align_bytes=64)
-        nc.scalar.copy(
-            w2_b[:].rearrange("p (c i) j -> p c j i", i=4), w2_raw[:].rearrange("p j (c i) -> p c j i", i=4)
-        )
 
         combine(*pending)
         z2_mx = mx_tiles("z2")
@@ -199,8 +199,7 @@ def tile_picked_fkcdnormbgapgmid_none_p_kernel(
         w2_s = keep.tile([P, N], U8, name="w2_s", align_bytes=64)
         z_f = keep.tile([P, TILES, S], F32, name="z_f", tag="z2_b1", align_bytes=64)
         for t in range(TILES):
-            first = y1[:, t, :] if t < 2 else y_win[t][:].indirect(n1_t[:])
-            nc.vector.tensor_tensor(z_f[:, t, :], first, minus_y2[:, t, :], ALU.add)
+            nc.vector.tensor_tensor(z_f[:, t, :], y1[:, t, :], y2[:, t, :], ALU.subtract)
         nc.vector.quantize_mx(w2_w[:].bitcast(FP8X4), w2_s[:], w2_b[:].rearrange("p c t -> p (c t)"))
         z_mx = mx_tiles("z")
         quantise_rows(z_mx, z_f, gn_t, "z_b")
@@ -209,9 +208,8 @@ def tile_picked_fkcdnormbgapgmid_none_p_kernel(
         for i in range(TILES):
             nc.scalar.activation(b_win[i][:, 0:S], b_ps[i][:], ACT.Abs)
 
-        def denominator(i):
-            b5 = ring.tile([P, S], F32, name="b5", bufs=4)
-            scalar_gather(b5[:], b_win[i], n5_t[:])
+        def denominator(i, b5):
+            scalar_gather(b5, b_win[i], n5_t[:])
             den = psum.tile([P, S], F32, name="bank%d" % (TILES + i))
             for j in range(TILES):
                 cols = slice(P * j, P * (j + 1))
@@ -219,12 +217,12 @@ def tile_picked_fkcdnormbgapgmid_none_p_kernel(
                 nc.tensor.matmul(den[:, cols], b5[:, cols], ident[:], start=False, stop=True, is_transpose=True)
             return den
 
-        def inverse_root(i):
+        def inverse_root(den):
             root = ring.tile([P, S], F32, name="root", bufs=4)
-            nc.scalar.activation(root[:], den_ps[i][:], ACT.Abs_reciprocal_sqrt, bias=0.5, scale=0.0625)
+            nc.scalar.activation(root[:], den[:], ACT.Abs_reciprocal_sqrt, bias=0.5, scale=0.0625)
             return root
 
-        def inverse(i, root):
+        def square(root):
             inv_t = ring.tile([P, S], F32, name="inv_t", bufs=4)
             nc.scalar.activation(inv_t[:], root[:], ACT.Square)
             return inv_t
@@ -236,43 +234,43 @@ def tile_picked_fkcdnormbgapgmid_none_p_kernel(
                 nc.tensor.transpose(inv[:, cols], inv_t[:, cols], ident[:])
             return inv
 
-        den_ps = [denominator(i) for i in range(TILES)]
-        roots = [inverse_root(0)]
-        invs_t = []
-        for i in range(TILES):
-            if i + 1 < TILES:
-                roots.append(inverse_root(i + 1))
-            invs_t.append(inverse(i, roots[i]))
+        def inverses(first, b5):
+            dens = [denominator(first + u, b5[:, u, :]) for u in range(2)]
+            roots = [inverse_root(den) for den in dens]
+            return [square(root) for root in roots]
 
+        b5_early = keep.tile([P, 2, S], F32, name="b5_early")
+        invs_t = inverses(0, b5_early)
         a_ps = [product("bank%d" % i, (w2_w, w2_s), i, z_mx) for i in range(TILES)]
         a4 = keep.tile([P, TILES, S], F32, name="a4")
         for i in range(TILES):
-            if i < 2:
-                nc.vector.tensor_copy(a_win[i][:, 0:S], a_ps[i][:])
-            else:
-                nc.scalar.copy(a_win[i][:, 0:S], a_ps[i][:])
+            nc.vector.tensor_copy(a_win[i][:, 0:S], a_ps[i][:])
+        b5_late = keep.tile([P, 2, S], F32, name="b5_late", tag="z_b1", align_bytes=64)
+        invs_t.extend(inverses(2, b5_late))
         invs = [turn_back(i, invs_t[i]) for i in range(TILES)]
         for i in range(TILES):
-            if i < 2:
-                for cols, part in halves:
-                    vector_gather(a4[:, i, cols], a_win[i], n4_t[:, part])
-            else:
-                scalar_gather(a4[:, i, :], a_win[i], n4_t[:])
+            gather = vector_gather if i < 2 else scalar_gather
+            for cols, part in halves:
+                gather(a4[:, i, cols], a_win[i], n4_t[:, part])
 
-        def numerator(i):
-            num = ring.tile([P, S], F32, name="num", bufs=4)
-            nc.vector.tensor_tensor(num[:], a_win[i][:, 0:S], a4[:, i, :], ALU.subtract)
-            return num
+        num = keep.tile([P, TILES, S], F32, name="num")
+        res = keep.tile([P, TILES, S], F32, name="res")
 
-        def finish(i, num, pieces):
-            res = ring.tile([P, S], F32, name="res", bufs=4)
-            for cols in pieces:
-                nc.vector.tensor_tensor(res[:, cols], num[:, cols], invs[i][:, cols], ALU.mult)
-                nc.sync.dma_start(out[P * i : P * (i + 1), cols], res[:, cols])
+        def numerator(i, cols):
+            nc.vector.tensor_tensor(num[:, i, cols], a_win[i][:, cols], a4[:, i, cols], ALU.subtract)
 
-        whole = [slice(0, S)]
-        nums = [numerator(0), numerator(1)]
-        finish(0, nums[0], whole)
-        finish(1, nums[1], whole)
-        finish(2, numerator(2), whole)
-        finish(3, numerator(3), [cols for cols, part in halves])
+        def finish(i, cols):
+            nc.vector.tensor_tensor(res[:, i, cols], num[:, i, cols], invs[i][:, cols], ALU.mult)
+            nc.sync.dma_start(out[P * i : P * (i + 1), cols], res[:, i, cols])
+
+        whole = slice(0, S)
+        numerator(0, whole)
+        numerator(1, whole)
+        finish(0, whole)
+        finish(1, whole)
+        numerator(2, whole)
+        numerator(3, halves[0][0])
+        finish(2, whole)
+        numerator(3, halves[1][0])
+        finish(3, halves[0][0])
+        finish(3, halves[1][0])

from contextlib import ExitStack

import concourse.mybir as mybir
from concourse.masks import make_identity

K, T, S, N, H, W, C = 512, 2048, 512, 512, 512, 2048, 512
FLOPS = 2 * K * H * S + 2 * H * N * S + 2 * K * C * S

F32 = mybir.dt.float32
BF16 = mybir.dt.bfloat16
I32 = mybir.dt.int32
U32 = mybir.dt.uint32
U16 = mybir.dt.uint16
U8 = mybir.dt.uint8
FP8X4 = mybir.dt.float8_e4m3fn_x4
ALU = mybir.AluOpType
ACT = mybir.ActivationFunctionType

P = 128
PACK = 4
TILES = 4
HALF = S // 2
WIN = 528
Y_WIN = 1040


def tile_picked_fkcdnormbgapgmid_none_p_kernel(
    tc, x_words, x_scales, w1, gn, w2, gs, offs, n1, n2, n3, cand, n4, n5, out
):
    nc = tc.nc
    with ExitStack() as ctx:
        keep = ctx.enter_context(tc.tile_pool(name="keep", bufs=1))
        ring = ctx.enter_context(tc.tile_pool(name="ring", bufs=2))
        psum = ctx.enter_context(tc.psum_pool(name="psum", bufs=1))

        def load_list(name, src):
            lst = keep.tile(list(src.shape), U16, name=name)
            nc.sync.dma_start(lst[:], src)
            return lst

        def mx_tiles(name):
            words = keep.tile([P, 512], U32, name=name + "_words", align_bytes=64)
            scales = keep.tile([P, 512], U8, name=name + "_scales", align_bytes=64)
            return words, scales

        xs = keep.tile([P, T], U8, name="xs", align_bytes=64)
        nc.gpsimd.memset(xs[:].bitcast(I32), 0)
        offs_t = load_list("offs_t", offs)
        cand_t = load_list("cand_t", cand)
        for q in range(4):
            nc.sync.dma_start(
                xs[32 * q : 32 * q + 4, :].bitcast(I32), x_scales[0, 4 * q : 4 * q + 4, :].bitcast(I32)
            )
        w1_raw = keep.tile([P, PACK, H], F32, name="w1_raw")
        nc.sync.dma_start(w1_raw[:], w1.rearrange("(p j) c -> p j c", j=PACK))
        xw = keep.tile([P, T], I32, name="xw", align_bytes=64)
        nc.sync.dma_start(xw[:], x_words[0].rearrange("p c r -> p (c r)").bitcast(I32))
        n3_t = load_list("n3_t", n3)
        w2_raw = keep.tile([P, PACK, N], F32, name="w2_raw")
        nc.sync.dma_start(w2_raw[:], w2.rearrange("(p j) c -> p j c", j=PACK))
        gs_t = keep.tile([P, PACK], F32, name="gs_t")
        nc.sync.dma_start(gs_t[:], gs.rearrange("(p t) o -> p (t o)", t=PACK))
        gn_t = keep.tile([P, PACK], F32, name="gn_t")
        nc.sync.dma_start(gn_t[:], gn.rearrange("(p t) o -> p (t o)", t=PACK))
        n2_t = load_list("n2_t", n2)
        n1_t = load_list("n1_t", n1)
        n4_t = load_list("n4_t", n4)
        n5_t = load_list("n5_t", n5)

        y_win = [keep.tile([P, Y_WIN], F32, name="y_win%d" % t) for t in range(TILES)]
        a_win = [keep.tile([P, WIN], F32, name="a_win%d" % i) for i in range(TILES)]
        b_win = [keep.tile([P, WIN], F32, name="b_win%d" % i) for i in range(TILES)]
        for win in y_win + a_win + b_win:
            nc.gpsimd.memset(win[:, S:], 0.0)
        ident = keep.tile([P, P], F32, name="ident")
        make_identity(nc, ident[:])
        warm = keep.tile([P, 1], F32, name="warm")
        nc.scalar.activation(warm[:], y_win[0][:, S : S + 1], ACT.Abs_reciprocal_sqrt, bias=0.5, scale=0.0625)

        xo_w, xo_s = mx_tiles("xo")
        xc_w, xc_s = mx_tiles("xc")
        nc.vector.tensor_copy(xo_s[:], xs[:].indirect(offs_t[:]))
        nc.vector.tensor_copy(xc_s[:], xs[:].indirect(cand_t[:]))
        w1_b = keep.tile([P, TILES, P, PACK], BF16, name="w1_b", align_bytes=64)
        for h, copy in enumerate((nc.scalar.copy, nc.vector.tensor_copy)):
            copy(
                w1_b[:, :, 64 * h : 64 * h + 64, :].rearrange("p t m j -> p m j t"),
                w1_raw[:, :, HALF * h : HALF * (h + 1)].rearrange("p j (m t) -> p m j t", t=TILES),
            )
        w1_mx = mx_tiles("w1")
        nc.vector.quantize_mx(w1_mx[0][:].bitcast(FP8X4), w1_mx[1][:], w1_b[:].rearrange("p t m j -> p (t m j)"))
        halves = [(slice(HALF * h, HALF * (h + 1)), slice(16 * h, 16 * h + 16)) for h in range(2)]
        for cols, part in halves:
            nc.vector.tensor_copy(xo_w[:, cols], xw[:].bitcast(U32).indirect(offs_t[:, part]))

        def product(bank, left, block, right, moving=slice(0, S)):
            cols = slice(P * block, P * (block + 1))
            acc = psum.tile([P, moving.stop - moving.start], F32, name=bank)
            nc.tensor.matmul_mx(
                acc[:],
                lhsT=left[0][:, cols].bitcast(FP8X4),
                lhsT_scale=left[1][:, cols],
                rhs=right[0][:, moving].bitcast(FP8X4),
                rhs_scale=right[1][:, moving],
                start=True,
                stop=True,
            )
            return acc

        def quantise_rows(mx, rows, gain, tag):
            staged = [
                keep.tile([P, HALF, PACK], BF16, name="%s%d" % (tag, h), tag="%s%d" % (tag, h), align_bytes=64)
                for h in range(2)
            ]
            for h, (cols, part) in enumerate(halves):
                nc.vector.tensor_tensor(
                    staged[h][:].rearrange("p (c i) t -> p c t i", i=2),
                    rows[:, :, cols].rearrange("p t (c i) -> p c t i", i=2),
                    gain[:].unsqueeze(1).unsqueeze(3).to_broadcast([P, HALF // 2, PACK, 2]),
                    ALU.mult,
                )
            for h, (cols, part) in enumerate(halves):
                nc.vector.quantize_mx(
                    mx[0][:, cols].bitcast(FP8X4), mx[1][:, cols], staged[h][:].rearrange("p c t -> p (c t)")
                )

        def scalar_gather(dst, window, offsets):
            nc.scalar.activation(dst, window[:].indirect(offsets), ACT.Copy)

        def vector_gather(dst, window, offsets):
            nc.vector.tensor_copy(dst, window[:].indirect(offsets))

        y0_ps = [product("bank%d" % (TILES * h), w1_mx, 0, (xo_w, xo_s), halves[h][0]) for h in range(2)]
        y_ps = {t: product("bank%d" % t, w1_mx, t, (xo_w, xo_s)) for t in range(1, TILES)}
        members = [
            keep.tile([P, HALF, 2, 2, 2], F32, name="members%d" % t, tag="members%d" % t, align_bytes=64)
            for t in range(TILES)
        ]

        def fetch_members(t):
            flat = members[t][:].rearrange("p c g a b -> p (c g a b)")
            split = W - S if t == 0 else W
            for first in range(0, split, 2 * S):
                last = min(first + 2 * S, split)
                scalar_gather(flat[:, first:last], y_win[t], n3_t[:, first // 16 : last // 16])
            if split < W:
                vector_gather(flat[:, split:W], y_win[t], n3_t[:, split // 16 : W // 16])
                nc.vector.tensor_copy(xc_w[:], xw[:].bitcast(U32).indirect(cand_t[:]))

        w2_b = keep.tile([P, N, PACK], BF16, name="w2_b", align_bytes=64)
        for cols, part in halves:
            nc.gpsimd.tensor_scalar(
                w2_b[:, cols, :], w2_raw[:, :, cols].rearrange("p j c -> p c j"), 1.0, 0.0, ALU.mult, ALU.add
            )
        z2_f = keep.tile([P, TILES, S], F32, name="z2_f")
        for h, (cols, part) in enumerate(halves):
            nc.scalar.copy(y_win[0][:, cols], y0_ps[h][:])
        for t in range(1, TILES):
            nc.vector.tensor_copy(y_win[t][:, 0:S], y_ps[t][:])

        def combine(t, largest, raised):
            nc.vector.scalar_tensor_tensor(z2_f[:, t, :], largest[:], -0.5, raised[:], ALU.mult, ALU.add)

        def fold_members(t, op, name):
            folded = ring.tile([P, HALF, 2, 2], F32, name=name)
            nc.vector.tensor_tensor(
                folded[:].rearrange("p c b g -> p c g b"), members[t][:, :, :, 0, :], members[t][:, :, :, 1, :], op
            )
            return folded

        def fold_pairs(folded, op, name):
            single = ring.tile([P, HALF, 2], F32, name=name)
            nc.vector.tensor_tensor(single[:], folded[:, :, 0, :], folded[:, :, 1, :], op)
            return single[:].rearrange("p c g -> p (c g)")

        pending = None
        for t in range(TILES):
            fetch_members(t)
            lo = fold_members(t, ALU.min, "lo")
            if t > 0:
                combine(*pending)
            hi = fold_members(t, ALU.max, "hi")
            mn = fold_pairs(lo, ALU.min, "mn")
            mx = fold_pairs(hi, ALU.max, "mx")
            up = ring.tile([P, S], F32, name="up")
            nc.vector.tensor_tensor(up[:], mn, y_win[t][:, 0:S], ALU.max)
            pending = (t, mx, up)

        y1 = keep.tile([P, TILES, S], F32, name="y1")
        y2 = keep.tile([P, TILES, S], F32, name="y2")
        for t in range(TILES):
            scalar_gather(y2[:, t, :], y_win[t], n2_t[:])
            scalar_gather(y1[:, t, :], y_win[t], n1_t[:])

        combine(*pending)
        z2_mx = mx_tiles("z2")
        quantise_rows(z2_mx, z2_f, gs_t, "z2_b")
        w2_w = keep.tile([P, N], U32, name="w2_w", tag="z2_b0", align_bytes=64)
        w2_s = keep.tile([P, N], U8, name="w2_s", align_bytes=64)
        z_f = keep.tile([P, TILES, S], F32, name="z_f", tag="z2_b1", align_bytes=64)
        for t in range(TILES):
            nc.vector.tensor_tensor(z_f[:, t, :], y1[:, t, :], y2[:, t, :], ALU.subtract)
        nc.vector.quantize_mx(w2_w[:].bitcast(FP8X4), w2_s[:], w2_b[:].rearrange("p c t -> p (c t)"))
        z_mx = mx_tiles("z")
        quantise_rows(z_mx, z_f, gn_t, "z_b")

        b_ps = [product("bank%d" % (TILES + i), (xc_w, xc_s), i, z2_mx) for i in range(TILES)]
        for i in range(TILES):
            nc.scalar.activation(b_win[i][:, 0:S], b_ps[i][:], ACT.Abs)

        def denominator(i, b5):
            scalar_gather(b5, b_win[i], n5_t[:])
            den = psum.tile([P, S], F32, name="bank%d" % (TILES + i))
            for j in range(TILES):
                cols = slice(P * j, P * (j + 1))
                nc.tensor.matmul(den[:, cols], b_win[i][:, cols], ident[:], start=True, stop=False, is_transpose=True)
                nc.tensor.matmul(den[:, cols], b5[:, cols], ident[:], start=False, stop=True, is_transpose=True)
            return den

        def inverse_root(den):
            root = ring.tile([P, S], F32, name="root", bufs=4)
            nc.scalar.activation(root[:], den[:], ACT.Abs_reciprocal_sqrt, bias=0.5, scale=0.0625)
            return root

        def square(root):
            inv_t = ring.tile([P, S], F32, name="inv_t", bufs=4)
            nc.scalar.activation(inv_t[:], root[:], ACT.Square)
            return inv_t

        def turn_back(i, inv_t):
            inv = psum.tile([P, S], F32, name="bank%d" % i)
            for j in range(TILES):
                cols = slice(P * j, P * (j + 1))
                nc.tensor.transpose(inv[:, cols], inv_t[:, cols], ident[:])
            return inv

        def inverses(first, b5):
            dens = [denominator(first + u, b5[:, u, :]) for u in range(2)]
            roots = [inverse_root(den) for den in dens]
            return [square(root) for root in roots]

        b5_early = keep.tile([P, 2, S], F32, name="b5_early")
        invs_t = inverses(0, b5_early)
        a_ps = [product("bank%d" % i, (w2_w, w2_s), i, z_mx) for i in range(TILES)]
        a4 = keep.tile([P, TILES, S], F32, name="a4")
        for i in range(TILES):
            nc.vector.tensor_copy(a_win[i][:, 0:S], a_ps[i][:])
        b5_late = keep.tile([P, 2, S], F32, name="b5_late", tag="z_b1", align_bytes=64)
        invs_t.extend(inverses(2, b5_late))
        invs = [turn_back(i, invs_t[i]) for i in range(TILES)]
        for i in range(TILES):
            gather = vector_gather if i < 2 else scalar_gather
            for cols, part in halves:
                gather(a4[:, i, cols], a_win[i], n4_t[:, part])

        num = keep.tile([P, TILES, S], F32, name="num")
        res = keep.tile([P, TILES, S], F32, name="res")

        def numerator(i, cols):
            nc.vector.tensor_tensor(num[:, i, cols], a_win[i][:, cols], a4[:, i, cols], ALU.subtract)

        def finish(i, cols):
            nc.vector.tensor_tensor(res[:, i, cols], num[:, i, cols], invs[i][:, cols], ALU.mult)
            nc.sync.dma_start(out[P * i : P * (i + 1), cols], res[:, i, cols])

        whole = slice(0, S)
        numerator(0, whole)
        numerator(1, whole)
        finish(0, whole)
        finish(1, whole)
        numerator(2, whole)
        numerator(3, halves[0][0])
        finish(2, whole)
        numerator(3, halves[1][0])
        finish(3, halves[0][0])
        finish(3, halves[1][0])
